import numpy as np
import ml_dtypes


def mxq(x, axis, fmt="e4m3"):
    dtype, down = {"e4m3": (ml_dtypes.float8_e4m3fn, 7), "e5m2": (ml_dtypes.float8_e5m2, 14)}[fmt]
    v = np.moveaxis(np.asarray(x, np.float32).astype(ml_dtypes.bfloat16).astype(np.float64), axis, -1)
    blocks = v.reshape(v.shape[:-1] + (-1, 32))
    amax = np.abs(blocks).max(-1, keepdims=True)
    byte = np.maximum(np.where(amax > 0, np.frexp(amax)[1] - 1 + 127, 0) - down, 1)
    scale = np.exp2(byte - 127.0)
    codes = (blocks / scale).astype(np.float32).astype(dtype).astype(np.float64)
    return np.moveaxis((codes * scale).reshape(v.shape), -1, axis)


WIDE = False


def mx_kscale(k):
    if not WIDE:
        return np.ones(k)
    levels = np.array([10, -10, 5, -5, 0])
    if k % 512:
        return np.exp2(np.random.permutation(np.resize(levels, k // 32))).repeat(32)
    a = np.empty((k // 512, 16))
    for p in range(k // 512):
        a[p, :8] = np.random.permutation(np.resize(levels, 8))
        for g in range(8):
            far = levels[np.abs(levels - a[p, g]) >= 10]
            a[p, g + 8] = far[np.random.randint(len(far))]
    return np.exp2(a.ravel()).repeat(32)


def f64(x):
    return np.asarray(x).astype(np.float64)


def striped(idx):
    return np.tile(idx.reshape(-1, 16).T, (8, 1)).astype(np.uint16)


def unstriped(offs):
    return offs[:16].T.reshape(-1).astype(np.int64)


E2M1 = np.array([0.0, 0.5, 1.0, 1.5, 2.0, 3.0, 4.0, 6.0, -0.0, -0.5, -1.0, -1.5, -2.0, -3.0, -4.0, -6.0])


def pack_weight(w, fmt):
    k, n = w.shape
    w = f64(np.asarray(w, np.float32).astype(ml_dtypes.bfloat16)).reshape(k // 32, 32, n)
    amax = np.abs(w).max(1)
    if fmt == "e4m3":
        byte = np.frexp(amax)[1] - 1 + 127 - 7
    else:
        mant, ex = np.frexp(amax / 6.0)
        byte = np.where(mant > 0.5, ex, ex - 1) + 127
    byte = np.clip(np.where(amax > 0, byte, 1), 1, 254)
    scaled = (w * np.exp2(127.0 - byte)[:, None, :]).reshape(k, n).astype(np.float32)
    by_word = np.ascontiguousarray(scaled.reshape(k // 512, 128, 4, n).transpose(0, 1, 3, 2))
    if fmt == "e4m3":
        words = by_word.astype(ml_dtypes.float8_e4m3fn).view(np.uint8)
    else:
        c = by_word.astype(ml_dtypes.float4_e2m1fn).view(np.uint8) & 0xF
        words = (c[..., 0::2] | (c[..., 1::2] << 4)).reshape(k // 512, 128, 2 * n)
    return np.ascontiguousarray(words), np.ascontiguousarray(byte.astype(np.uint8).reshape(k // 512, 16, n))


def unpack_weight(words, scales, fmt):
    g, _, n = scales.shape
    words = np.ascontiguousarray(words).reshape(g, 128, n, -1)
    if fmt == "e4m3":
        vals = words.view(ml_dtypes.float8_e4m3fn).astype(np.float64)
    else:
        nib = np.empty((g, 128, n, 4), np.uint8)
        nib[..., 0::2] = words & 0xF
        nib[..., 1::2] = words >> 4
        vals = E2M1[nib]
    vals = vals * np.repeat(np.exp2(scales.astype(np.float64) - 127.0), 8, axis=1)[..., None]
    return vals.transpose(0, 1, 3, 2).reshape(g * 512, n)


def planes(y):
    n, m = y.shape
    v = y.astype(np.float32).astype(ml_dtypes.bfloat16).astype(np.float64).reshape(n // 32, 32, m)
    top = np.abs(v).max(1)
    byte = np.clip(np.where(top > 0, np.frexp(top)[1] - 1 + 127 - 7, 1), 1, 254)
    codes = (v * np.exp2(127.0 - byte)[:, None, :]).reshape(n, m).astype(np.float32).astype(ml_dtypes.float8_e4m3fn).view(np.uint8)
    words = codes.reshape(n // 512, 128, 4, m).transpose(0, 1, 3, 2)
    return np.ascontiguousarray(words), np.ascontiguousarray(byte.astype(np.uint8).reshape(n // 512, 16, m))


def silu(v):
    return v / (1.0 + np.exp(-np.maximum(v, -700.0)))


K, T, E, C, D, H, N = 512, 1024, 4, 256, 128, 512, 512


def by_expert(wq, xq, C):
    return np.concatenate([wq[e].T @ xq[:, e * C:(e + 1) * C] for e in range(E)], axis=1)


def setup_inputs():
    n = np.random.standard_normal
    s = mx_kscale(K)
    u = mx_kscale(H)
    first = np.random.permutation(np.repeat(np.arange(E), C))
    slots1 = np.concatenate([np.random.permutation(np.flatnonzero(first == e)) for e in range(E)])
    free = np.ones(T, bool); slots2 = np.empty(E * D, np.int64)
    for e in np.random.permutation(E):
        pick = np.random.permutation(np.flatnonzero(free & (first != e)))[:D]; slots2[e * D:(e + 1) * D] = pick; free[pick] = False
    g1 = np.random.uniform(0.5, 1.0, T); g2 = 1.0 - g1
    x = pack_weight(n((K, T)) * s[:, None], "e4m3")
    w1 = [pack_weight(m, "e4m3") for m in n((E, K, H)) / np.sqrt(K) / s[None, :, None] * u]
    w2 = [pack_weight(m, "e4m3") for m in n((E, H, N)) / np.sqrt(H) / u[None, :, None]]
    return {
        "x_words": x[0],
        "x_scales": x[1],
        "w1_words": np.stack([m[0] for m in w1]),
        "w1_scales": np.stack([m[1] for m in w1]),
        "w2_words": np.stack([m[0] for m in w2]),
        "w2_scales": np.stack([m[1] for m in w2]),
        "gate1": (np.tile(g1[slots1], (128, 1))).astype(np.float32),
        "gate2": (np.tile(g2[slots2], (128, 1))).astype(np.float32),
        "offs": striped(slots1),
        "offs2": striped(slots2),
    }


def reference(x_words, x_scales, w1_words, w1_scales, w2_words, w2_scales, gate1, gate2, offs, offs2):
    w1 = np.stack([unpack_weight(w1_words[e], w1_scales[e], "e4m3") for e in range(E)])
    w2 = np.stack([unpack_weight(w2_words[e], w2_scales[e], "e4m3") for e in range(E)])
    idx, idx2 = unstriped(offs), unstriped(offs2)
    x = unpack_weight(x_words, x_scales, "e4m3")
    h = silu(by_expert(w1, x[:, idx], C))
    y = by_expert(w2, mxq(h, 0, "e4m3"), C)
    h = silu(by_expert(w1, x[:, idx2], D))
    z = by_expert(w2, mxq(h, 0, "e4m3"), D)
    out = np.zeros((N, T))
    out[:, idx] = f64(gate1[:1]) * y
    out[:, idx2] += f64(gate2[:1]) * z
    out_0 = out
    return (out_0,) + planes(out_0)

from contextlib import ExitStack

import concourse.mybir as mybir
from concourse.masks import make_identity

K, T, E, C, D, H, N = 512, 1024, 4, 256, 128, 512, 512
FLOPS = 2 * E * (C + D) * (K * H + H * N)

F32 = mybir.dt.float32
BF16 = mybir.dt.bfloat16
I32 = mybir.dt.int32
U32 = mybir.dt.uint32
U16 = mybir.dt.uint16
U8 = mybir.dt.uint8
FP8X4 = mybir.dt.float8_e4m3fn_x4
MULT = mybir.AluOpType.mult
ADD = mybir.AluOpType.add
SILU = mybir.ActivationFunctionType.Silu

P = 128
PACK = 4
SLOTS = C + D
HALF = T // 2
LIST = 16


def tile_moe_ada_mlp_silu_kernel(
    tc, x_words, x_scales, w1_words, w1_scales, w2_words, w2_scales, gate1, gate2, offs, offs2, out_0, out_1, out_2
):
    nc = tc.nc
    with ExitStack() as ctx:
        keep = ctx.enter_context(tc.tile_pool(name="keep", bufs=1))
        ring = ctx.enter_context(tc.tile_pool(name="ring", bufs=2))
        psum = ctx.enter_context(tc.psum_pool(name="psum", bufs=1))

        def sb(name, shape, dtype, tag=None):
            return keep.tile(shape, dtype, name=name, tag=tag or name, align_bytes=64)

        first = sb("first", [P, T // LIST], U16)
        second = sb("second", [P, E * D // LIST], U16)
        xw = sb("xw", [P, T], I32)
        xs = sb("xs", [P, T], U8)
        w1 = [sb(f"w1_{e}", [P, H], I32) for e in range(E)]
        w2_raw = [sb(f"w2raw_{e}", [P, N], I32) for e in range(E)]
        w2 = [sb(f"w2_{e}", [P, N], I32) for e in range(E)]
        w1s = sb("w1s", [P, H], U8)
        w2s_raw = sb("w2sraw", [P, N], U8)
        w2s = sb("w2s", [P, N], U8)
        g1 = sb("g1", [P, T], F32)
        g2 = sb("g2", [P, E * D], F32)
        ident = sb("ident", [P, P], F32)
        ywin = [sb(f"ywin{t}", [P, T], F32) for t in range(PACK)]
        zwin = [sb(f"zwin{t}", [P, T], F32) for t in range(PACK)]
        warm = sb("warm", [P, 1], F32)

        pre = [psum.tile([P, 512], F32, name=f"pre{i}") for i in range(2)]
        turn = [psum.tile([P, 512], F32, name=f"turn{i}") for i in range(2)]
        res = [psum.tile([P, 512], F32, name=f"res{i}") for i in range(1)]

        nc.vector.memset(xs[:].bitcast(I32), 0)
        nc.vector.memset(w1s[:].bitcast(I32), 0)
        nc.vector.memset(w2s_raw[:].bitcast(I32), 0)
        make_identity(nc, ident[:])
        for z in zwin:
            nc.gpsimd.memset(z[:], 0.0)

        def words(ap):
            return ap.rearrange("p n d -> p (n d)").bitcast(I32)

        def load_weight_scales(plane, scales):
            for q in range(4):
                nc.sync.dma_start(
                    out=plane[32 * q : 32 * q + 4 * E, :].bitcast(I32),
                    in_=scales[:, 0, 4 * q : 4 * q + 4, :].bitcast(I32),
                )

        nc.sync.dma_start(first[:], offs)
        for r in range(4):
            nc.scalar.dma_start(out=xs[r:P:32, :].bitcast(I32), in_=x_scales[0, r:16:4, :].bitcast(I32))
        nc.scalar.activation(warm[:], ident[:, 0:1], SILU)
        nc.sync.dma_start(out=xw[:], in_=words(x_words[0]))
        nc.sync.dma_start(second[:], offs2)
        nc.sync.dma_start(out=w1[0][:], in_=words(w1_words[0, 0]))
        load_weight_scales(w1s, w1_scales)
        nc.sync.dma_start(out=w1[1][:], in_=words(w1_words[1, 0]))
        nc.sync.dma_start(out=w2_raw[0][:], in_=words(w2_words[0, 0]))
        load_weight_scales(w2s_raw, w2_scales)
        nc.sync.dma_start(out=w1[2][:], in_=words(w1_words[2, 0]))
        nc.sync.dma_start(out=g1[:, :HALF], in_=gate1[:, :HALF])
        nc.sync.dma_start(out=g2[:], in_=gate2)
        nc.sync.dma_start(out=w1[3][:], in_=words(w1_words[3, 0]))
        for e in range(1, E):
            nc.sync.dma_start(out=w2_raw[e][:], in_=words(w2_words[e, 0]))
        nc.sync.dma_start(out=g1[:, HALF:], in_=gate1[:, HALF:])

        def first_list(a, n):
            return first[:, a // LIST : (a + n) // LIST]

        def second_list(a, n):
            return second[:, a // LIST : (a + n) // LIST]

        def gather(e, xg, xsg):
            nc.vector.tensor_copy(xsg[:, :C], xs[:].indirect(first_list(e * C, C)))
            nc.vector.tensor_copy(xg[:, :C], xw[:].bitcast(U32).indirect(first_list(e * C, C)))
            nc.vector.tensor_copy(xsg[:, C:], xs[:].indirect(second_list(e * D, D)))
            nc.vector.tensor_copy(xg[:, C:], xw[:].bitcast(U32).indirect(second_list(e * D, D)))

        def deal_w2(e):
            nc.vector.tensor_copy(
                out=w2[e][:].rearrange("p (t c i) -> p c t i", t=PACK, i=4),
                in_=w2_raw[e][:].rearrange("p (c i t) -> p c t i", t=PACK, i=4),
            )

        hc = [sb(f"hc{e}", [P, SLOTS], U32) for e in range(E)]
        hs = [sb(f"hs{e}", [P, SLOTS], U8) for e in range(E)]

        def layer1(e, xg, xsg):
            h_first = sb(f"hfirst{e}", [P, C * PACK], BF16)
            h_second = sb(f"hsecond{e}", [P, D * PACK], BF16)
            for b in range(SLOTS // P):
                n = e * (SLOTS // P) + b
                cols = slice(b * P, (b + 1) * P)
                a = pre[n % 2]
                nc.tensor.matmul_mx(
                    out=a[:], lhsT=xg[:, cols].bitcast(FP8X4), lhsT_scale=xsg[:, cols],
                    rhs=w1[e][:].bitcast(FP8X4), rhs_scale=w1s[4 * e : P, :], start=True, stop=True,
                )
                hb = ring.tile([P, H], BF16, name="hb", align_bytes=64)
                nc.scalar.activation(
                    hb[:].rearrange("s (u p j) -> s u p j", u=2, j=2),
                    a[:].rearrange("s (p u j) -> s u p j", u=2, j=2), SILU,
                )
                pairs = hb[:].bitcast(F32)
                ht = turn[n % 2]
                for u in range(2):
                    nc.tensor.transpose(ht[:, u * P : (u + 1) * P], pairs[:, u * P : (u + 1) * P], ident[:])
                dst = h_first[:, b * H : (b + 1) * H] if b < C // P else h_second[:]
                nc.scalar.copy(
                    dst.bitcast(F32).rearrange("p (s u) -> p s u", u=2),
                    ht[:, : 2 * P].rearrange("p (u s) -> p s u", u=2),
                )
            nc.vector.quantize_mx(out=hc[e][:, :C].bitcast(FP8X4), scales=hs[e][:, :C], in_=h_first[:])
            nc.vector.quantize_mx(out=hc[e][:, C:].bitcast(FP8X4), scales=hs[e][:, C:], in_=h_second[:])

        def layer2(dst, e, t, cols):
            rows = slice(t * P, (t + 1) * P)
            nc.tensor.matmul_mx(
                out=dst, lhsT=w2[e][:, rows].bitcast(FP8X4), lhsT_scale=w2s[4 * e : P, rows],
                rhs=hc[e][:, cols].bitcast(FP8X4), rhs_scale=hs[e][:, cols], start=True, stop=True,
            )

        def scatter_first(t, src, a, n):
            nc.vector.tensor_tensor(ywin[t][:].indirect(first_list(a, n)), src, g1[:, a : a + n], MULT)

        def scatter_second(t, src, a, n):
            nc.vector.tensor_tensor(zwin[t][:].indirect(second_list(a, n)), src, g2[:, a : a + n], MULT)

        def expert_rows(e, t, bank):
            layer2(bank[:, :C], e, t, slice(0, C))
            layer2(bank[:, C:SLOTS], e, t, slice(C, SLOTS))
            src = sb(f"src{e}_{t}", [P, SLOTS], F32)
            nc.scalar.copy(src[:], bank[:, :SLOTS])
            scatter_first(t, src[:, :C], e * C, C)
            scatter_second(t, src[:, C:], e * D, D)

        def first_pair(e0, t, bank):
            for j in range(2):
                layer2(bank[:, j * C : (j + 1) * C], e0 + j, t, slice(0, C))
            src = sb(f"srcy{e0}_{t}", [P, 2 * C], F32)
            nc.scalar.copy(src[:], bank[:])
            scatter_first(t, src[:], e0 * C, 2 * C)

        def second_all(t, bank):
            for e in range(E):
                layer2(bank[:, e * D : (e + 1) * D], e, t, slice(C, SLOTS))
            src = sb(f"srcz{t}", [P, E * D], F32)
            nc.scalar.copy(src[:], bank[:])
            scatter_second(t, src[:], 0, E * D)

        total = [sb(f"total{h}", [P, PACK, HALF], F32) for h in range(2)]
        grouped = [sb(f"grouped{h}", [P, HALF, PACK], BF16) for h in range(2)]
        out_rows = out_0.rearrange("(p t) c -> p t c", t=PACK)

        def add_on_tensor(t):
            for h in range(2):
                flipped = ring.tile([P, HALF], F32, name="flipped", align_bytes=64)
                for b in range(HALF // P):
                    cols = slice(h * HALF + b * P, h * HALF + (b + 1) * P)
                    part = turn[h][:, b * P : (b + 1) * P]
                    nc.tensor.matmul(part, ywin[t][:, cols], ident[:], start=True, stop=False, is_transpose=True)
                    nc.tensor.matmul(part, zwin[t][:, cols], ident[:], start=False, stop=True, is_transpose=True)
                nc.scalar.copy(flipped[:], turn[h][:])
                for b in range(HALF // P):
                    blk = slice(b * P, (b + 1) * P)
                    nc.tensor.transpose(pre[h][:, blk], flipped[:, blk], ident[:])
                nc.scalar.copy(total[h][:, t, :], pre[h][:])
                nc.sync.dma_start(out=out_rows[:, t, h * HALF : (h + 1) * HALF], in_=total[h][:, t, :])

        def round_pair(copy, h, t0):
            copy(grouped[h][:, :, t0 : t0 + 2], total[h][:, t0 : t0 + 2, :].rearrange("p t c -> p c t"))

        xg = [sb(f"xg{i}", [P, SLOTS], U32) for i in range(2)]
        xsg = [sb(f"xsg{i}", [P, SLOTS], U8) for i in range(2)]
        gather(0, xg[0], xsg[0])
        gather(1, xg[1], xsg[1])
        deal_w2(0)
        nc.vector.tensor_copy(
            out=w2s[:].rearrange("p (t m) -> p m t", t=PACK), in_=w2s_raw[:].rearrange("p (m t) -> p m t", t=PACK)
        )
        layer1(0, xg[0], xsg[0])
        gather(2, xg[0], xsg[0])
        xg_last = sb("xg_last", [P, SLOTS], U32, tag="hfirst0")
        xsg_last = sb("xsg_last", [P, SLOTS], U8, tag="hsecond0")
        gather(3, xg_last, xsg_last)
        expert_rows(0, 0, res[0])
        layer1(1, xg[1], xsg[1])
        deal_w2(1)
        expert_rows(0, 1, turn[1])
        layer1(2, xg[0], xsg[0])
        deal_w2(2)
        expert_rows(1, 0, turn[0])
        layer1(3, xg_last, xsg_last)
        deal_w2(3)
        expert_rows(1, 1, turn[1])
        expert_rows(2, 0, turn[0])
        expert_rows(3, 0, turn[1])
        expert_rows(2, 1, turn[0])
        expert_rows(3, 1, turn[1])
        first_pair(0, 2, turn[0])
        second_all(2, turn[1])
        first_pair(2, 2, turn[0])
        first_pair(0, 3, turn[1])
        second_all(3, turn[0])
        first_pair(2, 3, turn[1])
        add_on_tensor(0)
        add_on_tensor(1)
        for h in range(2):
            round_pair(nc.scalar.copy, h, 0)
        add_on_tensor(2)

        t = PACK - 1
        codes = [sb(f"codes{h}", [P, HALF], I32) for h in range(2)]
        scales = sb("scales", [P, T], U8)
        for h in range(2):
            cols = slice(h * HALF, (h + 1) * HALF)
            nc.vector.tensor_tensor(total[h][:, t, :], ywin[t][:, cols], zwin[t][:, cols], ADD)
            nc.sync.dma_start(out=out_rows[:, t, cols], in_=total[h][:, t, :])
        round_pair(nc.scalar.copy, 0, 2)
        round_pair(nc.vector.tensor_copy, 1, 2)
        for h in (1, 0):
            cols = slice(h * HALF, (h + 1) * HALF)
            nc.vector.quantize_mx(
                out=codes[h][:].bitcast(FP8X4), scales=scales[:, cols], in_=grouped[h][:].rearrange("p c t -> p (c t)")
            )
            nc.sync.dma_start(out=words(out_1[0])[:, cols], in_=codes[h][:])
        for r in range(4):
            queue = nc.scalar if r % 2 else nc.sync
            queue.dma_start(out=out_2[0, r:16:4, :].bitcast(I32), in_=scales[r:P:32, :].bitcast(I32))
